import numpy as np
import ml_dtypes


def mxq(x, axis, fmt="e4m3"):
    dtype, down = {"e4m3": (ml_dtypes.float8_e4m3fn, 7), "e5m2": (ml_dtypes.float8_e5m2, 14)}[fmt]
    v = np.moveaxis(np.asarray(x, np.float32).astype(ml_dtypes.bfloat16).astype(np.float64), axis, -1)
    blocks = v.reshape(v.shape[:-1] + (-1, 32))
    amax = np.abs(blocks).max(-1, keepdims=True)
    byte = np.maximum(np.where(amax > 0, np.frexp(amax)[1] - 1 + 127, 0) - down, 1)
    scale = np.exp2(byte - 127.0)
    codes = (blocks / scale).astype(np.float32).astype(dtype).astype(np.float64)
    return np.moveaxis((codes * scale).reshape(v.shape), -1, axis)


WIDE = False


def mx_kscale(k):
    if not WIDE:
        return np.ones(k)
    levels = np.array([10, -10, 5, -5, 0])
    if k % 512:
        return np.exp2(np.random.permutation(np.resize(levels, k // 32))).repeat(32)
    a = np.empty((k // 512, 16))
    for p in range(k // 512):
        a[p, :8] = np.random.permutation(np.resize(levels, 8))
        for g in range(8):
            far = levels[np.abs(levels - a[p, g]) >= 10]
            a[p, g + 8] = far[np.random.randint(len(far))]
    return np.exp2(a.ravel()).repeat(32)


def f64(x):
    return np.asarray(x).astype(np.float64)


def striped(idx):
    return np.tile(idx.reshape(-1, 16).T, (8, 1)).astype(np.uint16)


def unstriped(offs):
    return offs[:16].T.reshape(-1).astype(np.int64)


E2M1 = np.array([0.0, 0.5, 1.0, 1.5, 2.0, 3.0, 4.0, 6.0, -0.0, -0.5, -1.0, -1.5, -2.0, -3.0, -4.0, -6.0])


def pack_weight(w, fmt):
    k, n = w.shape
    w = f64(np.asarray(w, np.float32).astype(ml_dtypes.bfloat16)).reshape(k // 32, 32, n)
    amax = np.abs(w).max(1)
    if fmt == "e4m3":
        byte = np.frexp(amax)[1] - 1 + 127 - 7
    else:
        mant, ex = np.frexp(amax / 6.0)
        byte = np.where(mant > 0.5, ex, ex - 1) + 127
    byte = np.clip(np.where(amax > 0, byte, 1), 1, 254)
    scaled = (w * np.exp2(127.0 - byte)[:, None, :]).reshape(k, n).astype(np.float32)
    by_word = np.ascontiguousarray(scaled.reshape(k // 512, 128, 4, n).transpose(0, 1, 3, 2))
    if fmt == "e4m3":
        words = by_word.astype(ml_dtypes.float8_e4m3fn).view(np.uint8)
    else:
        c = by_word.astype(ml_dtypes.float4_e2m1fn).view(np.uint8) & 0xF
        words = (c[..., 0::2] | (c[..., 1::2] << 4)).reshape(k // 512, 128, 2 * n)
    return np.ascontiguousarray(words), np.ascontiguousarray(byte.astype(np.uint8).reshape(k // 512, 16, n))


def unpack_weight(words, scales, fmt):
    g, _, n = scales.shape
    words = np.ascontiguousarray(words).reshape(g, 128, n, -1)
    if fmt == "e4m3":
        vals = words.view(ml_dtypes.float8_e4m3fn).astype(np.float64)
    else:
        nib = np.empty((g, 128, n, 4), np.uint8)
        nib[..., 0::2] = words & 0xF
        nib[..., 1::2] = words >> 4
        vals = E2M1[nib]
    vals = vals * np.repeat(np.exp2(scales.astype(np.float64) - 127.0), 8, axis=1)[..., None]
    return vals.transpose(0, 1, 3, 2).reshape(g * 512, n)


def relu(v):
    return np.maximum(v, 0.0)


K, T, E, C, N = 512, 2048, 12, 128, 512
M = 512


def by_expert(wq, xq):
    return np.concatenate([wq[e].T @ xq[:, e * C:(e + 1) * C] for e in range(E)], axis=1)


def setup_inputs():
    n = np.random.standard_normal
    s = mx_kscale(K)[:, None]
    v = mx_kscale(N)
    x = pack_weight(n((K, T)) * s, "e4m3")
    return {
        "x_words": x[0],
        "x_scales": x[1],
        "w": (n((E, K, N)) / np.sqrt(K) / s[None] * v[None, None, :]).astype(np.float32),
        "b": (0.3 * n((N, E)) * v[:, None]).astype(np.float32),
        "wp": (n((N, M)) / np.sqrt(N) / v[:, None]).astype(np.float32),
        "gate": np.tile(np.random.uniform(0.2, 1.0, E * C), (N, 1)).astype(np.float32),
        "offs": striped(np.random.permutation(T)[:E * C]),
    }


def reference(x_words, x_scales, w, b, wp, gate, offs):
    idx = unstriped(offs)
    xq = unpack_weight(x_words, x_scales, "e4m3")[:, idx]
    y = by_expert(mxq(f64(w), 1, "e4m3"), xq)
    y = relu(y + np.repeat(f64(b), C, axis=1))
    c = np.zeros((N, T))
    c[:, idx] = f64(gate) * y
    return mxq(f64(wp), 0, "e4m3").T @ mxq(c, 0, "e4m3")

@@ -1,0 +1,203 @@
+from contextlib import ExitStack
+
+import concourse.mybir as mybir
+
+K, T, E, C, N, M = 512, 2048, 12, 128, 512, 512
+S = E * C
+P = 128
+PACK = 4
+FLOPS = 2 * K * N * S + 2 * N * M * T
+BYTES = 4 * P * T + 16 * T + 4 * (E * K * N + N * E + N * M + P * S + M * T) + 2 * P * (S // 16)
+
+F32 = mybir.dt.float32
+BF16 = mybir.dt.bfloat16
+I32 = mybir.dt.int32
+U32 = mybir.dt.uint32
+U16 = mybir.dt.uint16
+U8 = mybir.dt.uint8
+FP8X4 = mybir.dt.float8_e4m3fn_x4
+RELU = mybir.ActivationFunctionType.Relu
+MULT = mybir.AluOpType.mult
+
+GROUP = 2
+GS = GROUP * C
+GROUPS = E // GROUP
+F_TILES = M // P
+VECTOR_CASTS = (3,)
+SPLIT_CASTS = (1,)
+SCALAR_SHARE = 48
+VECTOR_GATES = (0, 1)
+BANK = 512
+
+
+def tile_moe_nxt_lin_relu_kernel(tc, x_words, x_scales, w, b, wp, gate, offs, out):
+    nc = tc.nc
+    with ExitStack() as ctx:
+        keep = ctx.enter_context(tc.tile_pool(name="keep", bufs=1))
+        ring = ctx.enter_context(tc.tile_pool(name="ring", bufs=3))
+        psum = ctx.enter_context(tc.psum_pool(name="psum", bufs=4))
+
+        offsets = keep.tile([P, S // 16], U16, name="offsets")
+        tok_words = keep.tile([P, T], I32, name="tok_words", align_bytes=64)
+        tok_scales = keep.tile([P, T], U8, name="tok_scales", align_bytes=64)
+        slot_words = keep.tile([P, S], U32, name="slot_words", align_bytes=64)
+        slot_scales = keep.tile([P, S], U8, name="slot_scales", align_bytes=64)
+        bias = keep.tile([P, PACK, E], F32, name="bias")
+        gates = keep.tile([P, S], F32, name="gates")
+        w_raw = [keep.tile([P, PACK, N], F32, name=f"w_raw{e}") for e in range(E)]
+        wp_raw = keep.tile([P, PACK, M], F32, name="wp_raw")
+        windows = [keep.tile([P, T], F32, name=f"window{f}", align_bytes=64) for f in range(F_TILES)]
+
+        nc.gpsimd.memset(tok_scales[:].bitcast(I32), 0)
+        nc.vector.memset(windows[0][:], 0.0)
+        nc.vector.memset(windows[1][:], 0.0)
+        nc.scalar.copy(windows[2][:], windows[0][:])
+        nc.scalar.copy(windows[3][:], windows[0][:])
+
+        def load_w(e):
+            nc.sync.dma_start(w_raw[e][:], w[e].rearrange("(p j) n -> p j n", j=PACK))
+
+        nc.sync.dma_start(offsets[:], offs)
+        for q in range(4):
+            nc.sync.dma_start(tok_scales[32 * q : 32 * q + 4, :].bitcast(I32), x_scales[0, 4 * q : 4 * q + 4, :].bitcast(I32))
+        nc.sync.dma_start(tok_words[:], x_words[0].rearrange("p t r -> p (t r)").bitcast(I32))
+        load_w(0)
+        load_w(1)
+        nc.sync.dma_start(bias[:], b.rearrange("(p t) e -> p t e", t=PACK))
+        nc.sync.dma_start(gates[:, 0 : 2 * GS], gate[0:P, 0 : 2 * GS])
+        nc.sync.dma_start(wp_raw[:], wp.rearrange("(p j) f -> p j f", j=PACK))
+        for e in range(2, E):
+            load_w(e)
+            if e == 4:
+                nc.sync.dma_start(gates[:, 2 * GS : S], gate[0:P, 2 * GS : S])
+
+        nc.vector.tensor_copy(slot_scales[:], tok_scales[:].indirect(offsets[:]))
+        nc.vector.tensor_copy(slot_words[:], tok_words[:].bitcast(U32).indirect(offsets[:]))
+
+        w_bf, ys, c_bf, res = {}, {}, {}, {}
+
+        def cast(e):
+            w_bf[e] = ring.tile([P, N * PACK], BF16, name="w_bf", align_bytes=64, bufs=6)
+            dst = w_bf[e][:].rearrange("p (t m j) -> p m j t", t=PACK, j=PACK)
+            src = w_raw[e][:].rearrange("p j (m t) -> p m j t", t=PACK)
+            if e in VECTOR_CASTS:
+                nc.vector.tensor_copy(dst, src)
+            elif e in SPLIT_CASTS:
+                nc.scalar.copy(dst[:, :SCALAR_SHARE], src[:, :SCALAR_SHARE])
+                nc.vector.tensor_copy(dst[:, SCALAR_SHARE:], src[:, SCALAR_SHARE:])
+            else:
+                nc.scalar.copy(dst, src)
+
+        def quantize(src, width, name):
+            codes = ring.tile([P, width], U32, name=name + "_codes", align_bytes=64)
+            scales = ring.tile([P, width], U8, name=name + "_scales", align_bytes=64)
+            nc.vector.quantize_mx(out=codes[:].bitcast(FP8X4), scales=scales[:], in_=src)
+            return codes, scales
+
+        def product(dst, lhs, lhs_cols, rhs, rhs_cols):
+            nc.tensor.matmul_mx(
+                out=dst,
+                lhsT=lhs[0][:, lhs_cols].bitcast(FP8X4),
+                lhsT_scale=lhs[1][:, lhs_cols],
+                rhs=rhs[0][:, rhs_cols].bitcast(FP8X4),
+                rhs_scale=rhs[1][:, rhs_cols],
+                start=True,
+                stop=True,
+            )
+
+        banks1, banks2, cqs = {}, {}, {}
+        last = GROUPS - 1
+
+        def expert(e):
+            wq = quantize(w_bf[e][:], N, "wq")
+            banks1[e] = psum.tile([P, BANK], F32, name="bank1")
+            for t in range(PACK):
+                product(banks1[e][:, t * C : (t + 1) * C], wq, slice(t * P, (t + 1) * P), (slot_words, slot_scales), slice(e * C, (e + 1) * C))
+
+        def activate(e):
+            g, h = divmod(e, GROUP)
+            y = ring.tile([P, PACK, C], F32, name="y", bufs=4)
+            for t in range(PACK):
+                nc.scalar.activation(y[:, t, :], banks1[e][:, t * C : (t + 1) * C], RELU, bias=bias[:, t, e : e + 1])
+            if h == 0:
+                c_bf[g] = ring.tile([P, GS * PACK], BF16, name="c_bf", align_bytes=64)
+            engine = nc.vector if e in VECTOR_GATES else nc.gpsimd
+            engine.tensor_tensor(
+                c_bf[g][:, h * C * PACK : (h + 1) * C * PACK].rearrange("p (j t) -> p j t", t=PACK),
+                y[:].rearrange("p t j -> p j t"),
+                gates[:, e * C : (e + 1) * C].unsqueeze(2).to_broadcast([P, C, PACK]),
+                MULT,
+            )
+
+        tail_codes = keep.tile([P, 2 * GS], U32, name="tail_codes", align_bytes=64)
+        tail_scales = keep.tile([P, 2 * GS], U8, name="tail_scales", align_bytes=64)
+
+        def project(g):
+            if g < last - 1:
+                cq = quantize(c_bf[g][:], GS, "cq")
+                cols = slice(0, GS)
+                halves = (0, 1)
+            else:
+                cols = slice((g - last + 1) * GS, (g - last + 2) * GS)
+                cq = (tail_codes, tail_scales)
+                nc.vector.quantize_mx(out=tail_codes[:, cols].bitcast(FP8X4), scales=tail_scales[:, cols], in_=c_bf[g][:])
+                halves = (0,)
+            for half in halves:
+                banks2[g, half] = psum.tile([P, BANK], F32, name="bank2")
+                for h in range(2):
+                    f = 2 * half + h
+                    product(banks2[g, half][:, h * GS : (h + 1) * GS], wpq, slice(f * P, (f + 1) * P), cq, cols)
+
+        def store(f):
+            nc.sync.dma_start(out[f * P : (f + 1) * P, :], windows[f][:])
+
+        def scatter(g, half):
+            res = ring.tile([P, BANK], F32, name="res", bufs=6)
+            nc.scalar.copy(res[:], banks2[g, half][:])
+            lst = offsets[:, g * GS // 16 : (g + 1) * GS // 16]
+            for h in range(2):
+                f = 2 * half + h
+                nc.vector.tensor_copy(windows[f][:].indirect(lst), res[:, h * GS : (h + 1) * GS])
+                if g == last:
+                    store(f)
+
+        def tail(f):
+            bank = psum.tile([P, BANK], F32, name="bank2")
+            product(bank[:], wpq, slice(f * P, (f + 1) * P), (tail_codes, tail_scales), slice(0, 2 * GS))
+            res = ring.tile([P, BANK], F32, name="res", bufs=6)
+            nc.scalar.copy(res[:], bank[:])
+            lst = offsets[:, (last - 1) * GS // 16 : S // 16]
+            nc.vector.tensor_copy(windows[f][:].indirect(lst), res[:])
+            store(f)
+
+        cast(0)
+        expert(0)
+        cast(1)
+        expert(1)
+        wp_bf = keep.tile([P, M * PACK], BF16, name="wp_bf", align_bytes=64)
+        nc.vector.tensor_copy(
+            wp_bf[:].rearrange("p (c i j) -> p c j i", i=4, j=PACK),
+            wp_raw[:].rearrange("p j (c i) -> p c j i", i=4),
+        )
+        wpq = quantize(wp_bf[:], M, "wpq")
+        activate(0)
+        activate(1)
+        project(0)
+        scatter(0, 0)
+        cast(2)
+        expert(2)
+        cast(3)
+        expert(3)
+        scatter(0, 1)
+        for e in range(4, E + 2):
+            if e < E:
+                cast(e)
+                expert(e)
+            activate(e - 2)
+            if e % 2 == 1:
+                project((e - 2) // 2)
+            if e >= 7:
+                scatter(*divmod(e - 5, 2))
+        scatter(last, 0)
+        tail(2)
+        tail(3)

@@ -6,8 +6,10 @@ K, T, E, C, N, M = 512, 2048, 12, 128, 512, 512
 S = E * C
 P = 128
 PACK = 4
+LIST_ROWS = 16
+BANK = 512
 FLOPS = 2 * K * N * S + 2 * N * M * T
-BYTES = 4 * P * T + 16 * T + 4 * (E * K * N + N * E + N * M + P * S + M * T) + 2 * P * (S // 16)
+BYTES = 4 * P * T + 16 * T + 4 * (E * K * N + N * E + N * M + P * S + M * T) + 2 * P * (S // LIST_ROWS)
 
 F32 = mybir.dt.float32
 BF16 = mybir.dt.bfloat16
@@ -19,185 +21,177 @@ FP8X4 = mybir.dt.float8_e4m3fn_x4
 RELU = mybir.ActivationFunctionType.Relu
 MULT = mybir.AluOpType.mult
 
-GROUP = 2
-GS = GROUP * C
-GROUPS = E // GROUP
+PAIR = 2 * C
+PAIRS = S // PAIR
 F_TILES = M // P
-VECTOR_CASTS = (3,)
-SPLIT_CASTS = (1,)
-SCALAR_SHARE = 48
-VECTOR_GATES = (0, 1)
-BANK = 512
+
+PRIMED = 4
+HALF = P // 2
+EARLY_TOKENS = T // 4
+
+PIECES = (
+    [[(0, 0, 1), (1, 0, 1)]]
+    + [[(f, g, 2)] for g in range(PAIRS - 2) for f in ((2, 3) if g % 2 == 0 else (0, 1))]
+    + [[(0, PAIRS - 1, 1), (1, PAIRS - 1, 1)], [(2, PAIRS - 2, 2)], [(3, PAIRS - 2, 2)]]
+)
+PIECE_LAG = PRIMED + 1
 
 
 def tile_moe_nxt_lin_relu_kernel(tc, x_words, x_scales, w, b, wp, gate, offs, out):
     nc = tc.nc
     with ExitStack() as ctx:
         keep = ctx.enter_context(tc.tile_pool(name="keep", bufs=1))
-        ring = ctx.enter_context(tc.tile_pool(name="ring", bufs=3))
+        ring = ctx.enter_context(tc.tile_pool(name="ring", bufs=4))
         psum = ctx.enter_context(tc.psum_pool(name="psum", bufs=4))
 
-        offsets = keep.tile([P, S // 16], U16, name="offsets")
-        tok_words = keep.tile([P, T], I32, name="tok_words", align_bytes=64)
-        tok_scales = keep.tile([P, T], U8, name="tok_scales", align_bytes=64)
+        offsets = keep.tile([P, S // LIST_ROWS], U16, name="offsets")
+        token_words = keep.tile([P, T], I32, name="token_words", align_bytes=64)
+        token_scales = keep.tile([P, T], U8, name="token_scales", align_bytes=64)
         slot_words = keep.tile([P, S], U32, name="slot_words", align_bytes=64)
         slot_scales = keep.tile([P, S], U8, name="slot_scales", align_bytes=64)
         bias = keep.tile([P, PACK, E], F32, name="bias")
         gates = keep.tile([P, S], F32, name="gates")
         w_raw = [keep.tile([P, PACK, N], F32, name=f"w_raw{e}") for e in range(E)]
         wp_raw = keep.tile([P, PACK, M], F32, name="wp_raw")
-        windows = [keep.tile([P, T], F32, name=f"window{f}", align_bytes=64) for f in range(F_TILES)]
+        wp_bf = keep.tile([P, M * PACK], BF16, name="wp_bf", align_bytes=64)
+        wp_words = keep.tile([P, M], U32, name="wp_words", align_bytes=64)
+        wp_scales = keep.tile([P, M], U8, name="wp_scales", align_bytes=64)
+        c_words = keep.tile([P, S], U32, name="c_words", align_bytes=64)
+        c_scales = keep.tile([P, S], U8, name="c_scales", align_bytes=64)
+        out_tiles = [keep.tile([P, T], F32, name=f"out_tile{f}", align_bytes=64) for f in range(F_TILES)]
 
-        nc.gpsimd.memset(tok_scales[:].bitcast(I32), 0)
-        nc.vector.memset(windows[0][:], 0.0)
-        nc.vector.memset(windows[1][:], 0.0)
-        nc.scalar.copy(windows[2][:], windows[0][:])
-        nc.scalar.copy(windows[3][:], windows[0][:])
+        nc.gpsimd.memset(token_scales[:].bitcast(I32), 0)
+        nc.vector.memset(out_tiles[0][:], 0.0)
+        nc.vector.memset(out_tiles[1][:], 0.0)
+        nc.scalar.copy(out_tiles[2][:], out_tiles[0][:])
+        nc.scalar.copy(out_tiles[3][:], out_tiles[0][:])
 
-        def load_w(e):
-            nc.sync.dma_start(w_raw[e][:], w[e].rearrange("(p j) n -> p j n", j=PACK))
+        def load_w(first, end):
+            for e in range(first, end):
+                nc.sync.dma_start(w_raw[e][:], w[e].rearrange("(p j) n -> p j n", j=PACK))
 
+        primed_slots = PRIMED * C
+        words_in = x_words[0].rearrange("p t r -> p (t r)").bitcast(I32)
         nc.sync.dma_start(offsets[:], offs)
-        for q in range(4):
-            nc.sync.dma_start(tok_scales[32 * q : 32 * q + 4, :].bitcast(I32), x_scales[0, 4 * q : 4 * q + 4, :].bitcast(I32))
-        nc.sync.dma_start(tok_words[:], x_words[0].rearrange("p t r -> p (t r)").bitcast(I32))
-        load_w(0)
-        load_w(1)
+        nc.sync.dma_start(token_words[:, :EARLY_TOKENS], words_in[:, :EARLY_TOKENS])
+        for quad in range(4):
+            nc.sync.dma_start(
+                token_scales[32 * quad : 32 * quad + 4, :].bitcast(I32),
+                x_scales[0, 4 * quad : 4 * quad + 4, :].bitcast(I32),
+            )
+        nc.sync.dma_start(token_words[:, EARLY_TOKENS:], words_in[:, EARLY_TOKENS:])
+        load_w(0, PRIMED)
         nc.sync.dma_start(bias[:], b.rearrange("(p t) e -> p t e", t=PACK))
-        nc.sync.dma_start(gates[:, 0 : 2 * GS], gate[0:P, 0 : 2 * GS])
+        nc.sync.dma_start(gates[:, :primed_slots], gate[0:P, :primed_slots])
         nc.sync.dma_start(wp_raw[:], wp.rearrange("(p j) f -> p j f", j=PACK))
-        for e in range(2, E):
-            load_w(e)
-            if e == 4:
-                nc.sync.dma_start(gates[:, 2 * GS : S], gate[0:P, 2 * GS : S])
+        nc.sync.dma_start(gates[:, primed_slots:], gate[0:P, primed_slots:])
+        load_w(PRIMED, E)
 
-        nc.vector.tensor_copy(slot_scales[:], tok_scales[:].indirect(offsets[:]))
-        nc.vector.tensor_copy(slot_words[:], tok_words[:].bitcast(U32).indirect(offsets[:]))
+        nc.vector.tensor_copy(slot_scales[:], token_scales[:].indirect(offsets[:]))
+        nc.vector.tensor_copy(slot_words[:], token_words[:].bitcast(U32).indirect(offsets[:]))
 
-        w_bf, ys, c_bf, res = {}, {}, {}, {}
-
-        def cast(e):
-            w_bf[e] = ring.tile([P, N * PACK], BF16, name="w_bf", align_bytes=64, bufs=6)
-            dst = w_bf[e][:].rearrange("p (t m j) -> p m j t", t=PACK, j=PACK)
-            src = w_raw[e][:].rearrange("p j (m t) -> p m j t", t=PACK)
-            if e in VECTOR_CASTS:
-                nc.vector.tensor_copy(dst, src)
-            elif e in SPLIT_CASTS:
-                nc.scalar.copy(dst[:, :SCALAR_SHARE], src[:, :SCALAR_SHARE])
-                nc.vector.tensor_copy(dst[:, SCALAR_SHARE:], src[:, SCALAR_SHARE:])
+        def round_copy(dst, src, shared):
+            if shared:
+                nc.scalar.copy(dst[:, :HALF], src[:, :HALF])
+                nc.vector.tensor_copy(dst[:, HALF:], src[:, HALF:])
             else:
                 nc.scalar.copy(dst, src)
 
-        def quantize(src, width, name):
-            codes = ring.tile([P, width], U32, name=name + "_codes", align_bytes=64)
-            scales = ring.tile([P, width], U8, name=name + "_scales", align_bytes=64)
-            nc.vector.quantize_mx(out=codes[:].bitcast(FP8X4), scales=scales[:], in_=src)
-            return codes, scales
+        def quantize(words, scales, values):
+            nc.vector.quantize_mx(out=words.bitcast(FP8X4), scales=scales, in_=values)
 
-        def product(dst, lhs, lhs_cols, rhs, rhs_cols):
+        def product(dst, lhs_words, lhs_scales, rhs_words, rhs_scales):
             nc.tensor.matmul_mx(
                 out=dst,
-                lhsT=lhs[0][:, lhs_cols].bitcast(FP8X4),
-                lhsT_scale=lhs[1][:, lhs_cols],
-                rhs=rhs[0][:, rhs_cols].bitcast(FP8X4),
-                rhs_scale=rhs[1][:, rhs_cols],
+                lhsT=lhs_words.bitcast(FP8X4),
+                lhsT_scale=lhs_scales,
+                rhs=rhs_words.bitcast(FP8X4),
+                rhs_scale=rhs_scales,
                 start=True,
                 stop=True,
             )
 
-        banks1, banks2, cqs = {}, {}, {}
-        last = GROUPS - 1
+        expert_banks, ys, c_bf = {}, {}, {}
 
-        def expert(e):
-            wq = quantize(w_bf[e][:], N, "wq")
-            banks1[e] = psum.tile([P, BANK], F32, name="bank1")
+        def expert_product(e):
+            w_bf = ring.tile([P, N * PACK], BF16, name="w_bf", align_bytes=64)
+            round_copy(
+                w_bf[:].rearrange("p (t m j) -> p m j t", t=PACK, j=PACK),
+                w_raw[e][:].rearrange("p j (m t) -> p m j t", t=PACK),
+                shared=0 < e < PRIMED or e % 2 == 1,
+            )
+            w_words = ring.tile([P, N], U32, name="w_words", align_bytes=64)
+            w_scales = ring.tile([P, N], U8, name="w_scales", align_bytes=64)
+            quantize(w_words[:], w_scales[:], w_bf[:])
+            expert_banks[e] = psum.tile([P, PACK, C], F32, name="expert_bank")
+            slots = slice(e * C, (e + 1) * C)
             for t in range(PACK):
-                product(banks1[e][:, t * C : (t + 1) * C], wq, slice(t * P, (t + 1) * P), (slot_words, slot_scales), slice(e * C, (e + 1) * C))
+                cols = slice(t * P, (t + 1) * P)
+                product(expert_banks[e][:, t, :], w_words[:, cols], w_scales[:, cols], slot_words[:, slots], slot_scales[:, slots])
 
         def activate(e):
-            g, h = divmod(e, GROUP)
-            y = ring.tile([P, PACK, C], F32, name="y", bufs=4)
+            ys[e] = ring.tile([P, PACK * C], F32, name="y")
             for t in range(PACK):
-                nc.scalar.activation(y[:, t, :], banks1[e][:, t * C : (t + 1) * C], RELU, bias=bias[:, t, e : e + 1])
-            if h == 0:
-                c_bf[g] = ring.tile([P, GS * PACK], BF16, name="c_bf", align_bytes=64)
-            engine = nc.vector if e in VECTOR_GATES else nc.gpsimd
-            engine.tensor_tensor(
-                c_bf[g][:, h * C * PACK : (h + 1) * C * PACK].rearrange("p (j t) -> p j t", t=PACK),
-                y[:].rearrange("p t j -> p j t"),
+                nc.scalar.activation(ys[e][:, t * C : (t + 1) * C], expert_banks[e][:, t, :], RELU, bias=bias[:, t, e : e + 1])
+            g, half = divmod(e, 2)
+            if half == 0:
+                c_bf[g] = ring.tile([P, 2, C * PACK], BF16, name="c_bf", align_bytes=64)
+            nc.vector.tensor_tensor(
+                c_bf[g][:, half, :].rearrange("p (j t) -> p j t", t=PACK),
+                ys[e][:].rearrange("p (t j) -> p j t", t=PACK),
                 gates[:, e * C : (e + 1) * C].unsqueeze(2).to_broadcast([P, C, PACK]),
                 MULT,
             )
 
-        tail_codes = keep.tile([P, 2 * GS], U32, name="tail_codes", align_bytes=64)
-        tail_scales = keep.tile([P, 2 * GS], U8, name="tail_scales", align_bytes=64)
+        def quantize_c(g):
+            slots = slice(g * PAIR, (g + 1) * PAIR)
+            quantize(c_words[:, slots], c_scales[:, slots], c_bf[g][:].rearrange("p h x -> p (h x)"))
 
-        def project(g):
-            if g < last - 1:
-                cq = quantize(c_bf[g][:], GS, "cq")
-                cols = slice(0, GS)
-                halves = (0, 1)
-            else:
-                cols = slice((g - last + 1) * GS, (g - last + 2) * GS)
-                cq = (tail_codes, tail_scales)
-                nc.vector.quantize_mx(out=tail_codes[:, cols].bitcast(FP8X4), scales=tail_scales[:, cols], in_=c_bf[g][:])
-                halves = (0,)
-            for half in halves:
-                banks2[g, half] = psum.tile([P, BANK], F32, name="bank2")
-                for h in range(2):
-                    f = 2 * half + h
-                    product(banks2[g, half][:, h * GS : (h + 1) * GS], wpq, slice(f * P, (f + 1) * P), cq, cols)
+        def staging(k):
+            if k + PRIMED < E:
+                return w_raw[k + PRIMED][:, 0, :]
+            if k + PRIMED == E:
+                return ys[E - 1][:]
+            staged = ring.tile([P, BANK], F32, name="staged")
+            return staged[:]
 
-        def store(f):
-            nc.sync.dma_start(out[f * P : (f + 1) * P, :], windows[f][:])
+        def piece(k):
+            bank = psum.tile([P, BANK], F32, name="projection_bank")
+            parts, col = [], 0
+            for f, g, count in PIECES[k]:
+                slots = slice(g * PAIR, (g + count) * PAIR)
+                cols = slice(col, col + count * PAIR)
+                features = slice(f * P, (f + 1) * P)
+                product(bank[:, cols], wp_words[:, features], wp_scales[:, features], c_words[:, slots], c_scales[:, slots])
+                parts.append((f, slots, cols))
+                col = cols.stop
+            sums = staging(k)
+            nc.scalar.copy(sums, bank[:])
+            for f, slots, cols in parts:
+                entries = offsets[:, slots.start // LIST_ROWS : slots.stop // LIST_ROWS]
+                nc.vector.tensor_copy(out_tiles[f][:].indirect(entries), sums[:, cols])
+                if slots.stop == S:
+                    nc.sync.dma_start(out[f * P : (f + 1) * P, :], out_tiles[f][:])
 
-        def scatter(g, half):
-            res = ring.tile([P, BANK], F32, name="res", bufs=6)
-            nc.scalar.copy(res[:], banks2[g, half][:])
-            lst = offsets[:, g * GS // 16 : (g + 1) * GS // 16]
-            for h in range(2):
-                f = 2 * half + h
-                nc.vector.tensor_copy(windows[f][:].indirect(lst), res[:, h * GS : (h + 1) * GS])
-                if g == last:
-                    store(f)
-
-        def tail(f):
-            bank = psum.tile([P, BANK], F32, name="bank2")
-            product(bank[:], wpq, slice(f * P, (f + 1) * P), (tail_codes, tail_scales), slice(0, 2 * GS))
-            res = ring.tile([P, BANK], F32, name="res", bufs=6)
-            nc.scalar.copy(res[:], bank[:])
-            lst = offsets[:, (last - 1) * GS // 16 : S // 16]
-            nc.vector.tensor_copy(windows[f][:].indirect(lst), res[:])
-            store(f)
-
-        cast(0)
-        expert(0)
-        cast(1)
-        expert(1)
-        wp_bf = keep.tile([P, M * PACK], BF16, name="wp_bf", align_bytes=64)
-        nc.vector.tensor_copy(
+        for e in range(PRIMED):
+            expert_product(e)
+        round_copy(
             wp_bf[:].rearrange("p (c i j) -> p c j i", i=4, j=PACK),
             wp_raw[:].rearrange("p j (c i) -> p c j i", i=4),
+            shared=True,
         )
-        wpq = quantize(wp_bf[:], M, "wpq")
-        activate(0)
-        activate(1)
-        project(0)
-        scatter(0, 0)
-        cast(2)
-        expert(2)
-        cast(3)
-        expert(3)
-        scatter(0, 1)
-        for e in range(4, E + 2):
-            if e < E:
-                cast(e)
-                expert(e)
-            activate(e - 2)
-            if e % 2 == 1:
-                project((e - 2) // 2)
-            if e >= 7:
-                scatter(*divmod(e - 5, 2))
-        scatter(last, 0)
-        tail(2)
-        tail(3)
+        for e in range(PRIMED):
+            activate(e)
+        quantize(wp_words[:], wp_scales[:], wp_bf[:])
+        for g in range(PRIMED // 2):
+            quantize_c(g)
+
+        for step in range(PRIMED, len(PIECES) + PIECE_LAG):
+            if step < E:
+                expert_product(step)
+            if step >= PIECE_LAG:
+                piece(step - PIECE_LAG)
+            if PRIMED < step <= E:
+                activate(step - 1)
+                if step % 2 == 0:
+                    quantize_c(step // 2 - 1)

@@ -60,11 +60,12 @@ def tile_moe_nxt_lin_relu_kernel(tc, x_words, x_scales, w, b, wp, gate, offs, ou
         c_scales = keep.tile([P, S], U8, name="c_scales", align_bytes=64)
         out_tiles = [keep.tile([P, T], F32, name=f"out_tile{f}", align_bytes=64) for f in range(F_TILES)]
 
-        nc.gpsimd.memset(token_scales[:].bitcast(I32), 0)
+        zero = keep.tile([P, 1], F32, name="zero")
+        nc.gpsimd.memset(zero[:], 0.0)
         nc.vector.memset(out_tiles[0][:], 0.0)
-        nc.vector.memset(out_tiles[1][:], 0.0)
-        nc.scalar.copy(out_tiles[2][:], out_tiles[0][:])
-        nc.scalar.copy(out_tiles[3][:], out_tiles[0][:])
+        for f in range(1, F_TILES):
+            nc.scalar.copy(out_tiles[f][:], zero[:].to_broadcast([P, T]))
+        nc.gpsimd.memset(token_scales[:].bitcast(I32), 0)
 
         def load_w(first, end):
             for e in range(first, end):
@@ -84,8 +85,9 @@ def tile_moe_nxt_lin_relu_kernel(tc, x_words, x_scales, w, b, wp, gate, offs, ou
         nc.sync.dma_start(bias[:], b.rearrange("(p t) e -> p t e", t=PACK))
         nc.sync.dma_start(gates[:, :primed_slots], gate[0:P, :primed_slots])
         nc.sync.dma_start(wp_raw[:], wp.rearrange("(p j) f -> p j f", j=PACK))
+        load_w(PRIMED, PRIMED + 2)
         nc.sync.dma_start(gates[:, primed_slots:], gate[0:P, primed_slots:])
-        load_w(PRIMED, E)
+        load_w(PRIMED + 2, E)
 
         nc.vector.tensor_copy(slot_scales[:], token_scales[:].indirect(offsets[:]))
         nc.vector.tensor_copy(slot_words[:], token_words[:].bitcast(U32).indirect(offsets[:]))
@@ -118,7 +120,7 @@ def tile_moe_nxt_lin_relu_kernel(tc, x_words, x_scales, w, b, wp, gate, offs, ou
             round_copy(
                 w_bf[:].rearrange("p (t m j) -> p m j t", t=PACK, j=PACK),
                 w_raw[e][:].rearrange("p j (m t) -> p m j t", t=PACK),
-                shared=0 < e < PRIMED or e % 2 == 1,
+                shared=0 < e < PRIMED,
             )
             w_words = ring.tile([P, N], U32, name="w_words", align_bytes=64)
             w_scales = ring.tile([P, N], U8, name="w_scales", align_bytes=64)
@@ -136,7 +138,8 @@ def tile_moe_nxt_lin_relu_kernel(tc, x_words, x_scales, w, b, wp, gate, offs, ou
             g, half = divmod(e, 2)
             if half == 0:
                 c_bf[g] = ring.tile([P, 2, C * PACK], BF16, name="c_bf", align_bytes=64)
-            nc.vector.tensor_tensor(
+            engine = nc.vector if e < PRIMED else nc.gpsimd
+            engine.tensor_tensor(
                 c_bf[g][:, half, :].rearrange("p (j t) -> p j t", t=PACK),
                 ys[e][:].rearrange("p (t j) -> p j t", t=PACK),
                 gates[:, e * C : (e + 1) * C].unsqueeze(2).to_broadcast([P, C, PACK]),

from contextlib import ExitStack

import concourse.mybir as mybir

K, T, E, C, N, M = 512, 2048, 12, 128, 512, 512
S = E * C
P = 128
PACK = 4
LIST_ROWS = 16
BANK = 512
FLOPS = 2 * K * N * S + 2 * N * M * T
BYTES = 4 * P * T + 16 * T + 4 * (E * K * N + N * E + N * M + P * S + M * T) + 2 * P * (S // LIST_ROWS)

F32 = mybir.dt.float32
BF16 = mybir.dt.bfloat16
I32 = mybir.dt.int32
U32 = mybir.dt.uint32
U16 = mybir.dt.uint16
U8 = mybir.dt.uint8
FP8X4 = mybir.dt.float8_e4m3fn_x4
RELU = mybir.ActivationFunctionType.Relu
MULT = mybir.AluOpType.mult

PAIR = 2 * C
PAIRS = S // PAIR
F_TILES = M // P

PRIMED = 4
HALF = P // 2
EARLY_TOKENS = T // 4

PIECES = (
    [[(0, 0, 1), (1, 0, 1)]]
    + [[(f, g, 2)] for g in range(PAIRS - 2) for f in ((2, 3) if g % 2 == 0 else (0, 1))]
    + [[(0, PAIRS - 1, 1), (1, PAIRS - 1, 1)], [(2, PAIRS - 2, 2)], [(3, PAIRS - 2, 2)]]
)
PIECE_LAG = PRIMED + 1


def tile_moe_nxt_lin_relu_kernel(tc, x_words, x_scales, w, b, wp, gate, offs, out):
    nc = tc.nc
    with ExitStack() as ctx:
        keep = ctx.enter_context(tc.tile_pool(name="keep", bufs=1))
        ring = ctx.enter_context(tc.tile_pool(name="ring", bufs=4))
        psum = ctx.enter_context(tc.psum_pool(name="psum", bufs=4))

        offsets = keep.tile([P, S // LIST_ROWS], U16, name="offsets")
        token_words = keep.tile([P, T], I32, name="token_words", align_bytes=64)
        token_scales = keep.tile([P, T], U8, name="token_scales", align_bytes=64)
        slot_words = keep.tile([P, S], U32, name="slot_words", align_bytes=64)
        slot_scales = keep.tile([P, S], U8, name="slot_scales", align_bytes=64)
        bias = keep.tile([P, PACK, E], F32, name="bias")
        gates = keep.tile([P, S], F32, name="gates")
        w_raw = [keep.tile([P, PACK, N], F32, name=f"w_raw{e}") for e in range(E)]
        wp_raw = keep.tile([P, PACK, M], F32, name="wp_raw")
        wp_bf = keep.tile([P, M * PACK], BF16, name="wp_bf", align_bytes=64)
        wp_words = keep.tile([P, M], U32, name="wp_words", align_bytes=64)
        wp_scales = keep.tile([P, M], U8, name="wp_scales", align_bytes=64)
        c_words = keep.tile([P, S], U32, name="c_words", align_bytes=64)
        c_scales = keep.tile([P, S], U8, name="c_scales", align_bytes=64)
        out_tiles = [keep.tile([P, T], F32, name=f"out_tile{f}", align_bytes=64) for f in range(F_TILES)]

        zero = keep.tile([P, 1], F32, name="zero")
        nc.gpsimd.memset(zero[:], 0.0)
        nc.vector.memset(out_tiles[0][:], 0.0)
        for f in range(1, F_TILES):
            nc.scalar.copy(out_tiles[f][:], zero[:].to_broadcast([P, T]))
        nc.gpsimd.memset(token_scales[:].bitcast(I32), 0)

        def load_w(first, end):
            for e in range(first, end):
                nc.sync.dma_start(w_raw[e][:], w[e].rearrange("(p j) n -> p j n", j=PACK))

        primed_slots = PRIMED * C
        words_in = x_words[0].rearrange("p t r -> p (t r)").bitcast(I32)
        nc.sync.dma_start(offsets[:], offs)
        nc.sync.dma_start(token_words[:, :EARLY_TOKENS], words_in[:, :EARLY_TOKENS])
        for quad in range(4):
            nc.sync.dma_start(
                token_scales[32 * quad : 32 * quad + 4, :].bitcast(I32),
                x_scales[0, 4 * quad : 4 * quad + 4, :].bitcast(I32),
            )
        nc.sync.dma_start(token_words[:, EARLY_TOKENS:], words_in[:, EARLY_TOKENS:])
        load_w(0, PRIMED)
        nc.sync.dma_start(bias[:], b.rearrange("(p t) e -> p t e", t=PACK))
        nc.sync.dma_start(gates[:, :primed_slots], gate[0:P, :primed_slots])
        nc.sync.dma_start(wp_raw[:], wp.rearrange("(p j) f -> p j f", j=PACK))
        load_w(PRIMED, PRIMED + 2)
        nc.sync.dma_start(gates[:, primed_slots:], gate[0:P, primed_slots:])
        load_w(PRIMED + 2, E)

        nc.vector.tensor_copy(slot_scales[:], token_scales[:].indirect(offsets[:]))
        nc.vector.tensor_copy(slot_words[:], token_words[:].bitcast(U32).indirect(offsets[:]))

        def round_copy(dst, src, shared):
            if shared:
                nc.scalar.copy(dst[:, :HALF], src[:, :HALF])
                nc.vector.tensor_copy(dst[:, HALF:], src[:, HALF:])
            else:
                nc.scalar.copy(dst, src)

        def quantize(words, scales, values):
            nc.vector.quantize_mx(out=words.bitcast(FP8X4), scales=scales, in_=values)

        def product(dst, lhs_words, lhs_scales, rhs_words, rhs_scales):
            nc.tensor.matmul_mx(
                out=dst,
                lhsT=lhs_words.bitcast(FP8X4),
                lhsT_scale=lhs_scales,
                rhs=rhs_words.bitcast(FP8X4),
                rhs_scale=rhs_scales,
                start=True,
                stop=True,
            )

        expert_banks, ys, c_bf = {}, {}, {}

        def expert_product(e):
            w_bf = ring.tile([P, N * PACK], BF16, name="w_bf", align_bytes=64)
            round_copy(
                w_bf[:].rearrange("p (t m j) -> p m j t", t=PACK, j=PACK),
                w_raw[e][:].rearrange("p j (m t) -> p m j t", t=PACK),
                shared=0 < e < PRIMED,
            )
            w_words = ring.tile([P, N], U32, name="w_words", align_bytes=64)
            w_scales = ring.tile([P, N], U8, name="w_scales", align_bytes=64)
            quantize(w_words[:], w_scales[:], w_bf[:])
            expert_banks[e] = psum.tile([P, PACK, C], F32, name="expert_bank")
            slots = slice(e * C, (e + 1) * C)
            for t in range(PACK):
                cols = slice(t * P, (t + 1) * P)
                product(expert_banks[e][:, t, :], w_words[:, cols], w_scales[:, cols], slot_words[:, slots], slot_scales[:, slots])

        def activate(e):
            ys[e] = ring.tile([P, PACK * C], F32, name="y")
            for t in range(PACK):
                nc.scalar.activation(ys[e][:, t * C : (t + 1) * C], expert_banks[e][:, t, :], RELU, bias=bias[:, t, e : e + 1])
            g, half = divmod(e, 2)
            if half == 0:
                c_bf[g] = ring.tile([P, 2, C * PACK], BF16, name="c_bf", align_bytes=64)
            engine = nc.vector if e < PRIMED else nc.gpsimd
            engine.tensor_tensor(
                c_bf[g][:, half, :].rearrange("p (j t) -> p j t", t=PACK),
                ys[e][:].rearrange("p (t j) -> p j t", t=PACK),
                gates[:, e * C : (e + 1) * C].unsqueeze(2).to_broadcast([P, C, PACK]),
                MULT,
            )

        def quantize_c(g):
            slots = slice(g * PAIR, (g + 1) * PAIR)
            quantize(c_words[:, slots], c_scales[:, slots], c_bf[g][:].rearrange("p h x -> p (h x)"))

        def staging(k):
            if k + PRIMED < E:
                return w_raw[k + PRIMED][:, 0, :]
            if k + PRIMED == E:
                return ys[E - 1][:]
            staged = ring.tile([P, BANK], F32, name="staged")
            return staged[:]

        def piece(k):
            bank = psum.tile([P, BANK], F32, name="projection_bank")
            parts, col = [], 0
            for f, g, count in PIECES[k]:
                slots = slice(g * PAIR, (g + count) * PAIR)
                cols = slice(col, col + count * PAIR)
                features = slice(f * P, (f + 1) * P)
                product(bank[:, cols], wp_words[:, features], wp_scales[:, features], c_words[:, slots], c_scales[:, slots])
                parts.append((f, slots, cols))
                col = cols.stop
            sums = staging(k)
            nc.scalar.copy(sums, bank[:])
            for f, slots, cols in parts:
                entries = offsets[:, slots.start // LIST_ROWS : slots.stop // LIST_ROWS]
                nc.vector.tensor_copy(out_tiles[f][:].indirect(entries), sums[:, cols])
                if slots.stop == S:
                    nc.sync.dma_start(out[f * P : (f + 1) * P, :], out_tiles[f][:])

        for e in range(PRIMED):
            expert_product(e)
        round_copy(
            wp_bf[:].rearrange("p (c i j) -> p c j i", i=4, j=PACK),
            wp_raw[:].rearrange("p j (c i) -> p c j i", i=4),
            shared=True,
        )
        for e in range(PRIMED):
            activate(e)
        quantize(wp_words[:], wp_scales[:], wp_bf[:])
        for g in range(PRIMED // 2):
            quantize_c(g)

        for step in range(PRIMED, len(PIECES) + PIECE_LAG):
            if step < E:
                expert_product(step)
            if step >= PIECE_LAG:
                piece(step - PIECE_LAG)
            if PRIMED < step <= E:
                activate(step - 1)
                if step % 2 == 0:
                    quantize_c(step // 2 - 1)
